import numpy as np
import ml_dtypes


def mxq(x, axis, fmt="e4m3"):
    dtype, down = {"e4m3": (ml_dtypes.float8_e4m3fn, 7), "e5m2": (ml_dtypes.float8_e5m2, 14)}[fmt]
    v = np.moveaxis(np.asarray(x, np.float32).astype(ml_dtypes.bfloat16).astype(np.float64), axis, -1)
    blocks = v.reshape(v.shape[:-1] + (-1, 32))
    amax = np.abs(blocks).max(-1, keepdims=True)
    byte = np.maximum(np.where(amax > 0, np.frexp(amax)[1] - 1 + 127, 0) - down, 1)
    scale = np.exp2(byte - 127.0)
    codes = (blocks / scale).astype(np.float32).astype(dtype).astype(np.float64)
    return np.moveaxis((codes * scale).reshape(v.shape), -1, axis)


WIDE = False


def mx_kscale(k):
    if not WIDE:
        return np.ones(k)
    levels = np.array([10, -10, 5, -5, 0])
    if k % 512:
        return np.exp2(np.random.permutation(np.resize(levels, k // 32))).repeat(32)
    a = np.empty((k // 512, 16))
    for p in range(k // 512):
        a[p, :8] = np.random.permutation(np.resize(levels, 8))
        for g in range(8):
            far = levels[np.abs(levels - a[p, g]) >= 10]
            a[p, g + 8] = far[np.random.randint(len(far))]
    return np.exp2(a.ravel()).repeat(32)


def f64(x):
    return np.asarray(x).astype(np.float64)


def striped8(idx):
    return np.asarray(idx).reshape(8, -1, 16).transpose(0, 2, 1).reshape(128, -1).astype(np.uint16)


def unstriped8(offs):
    return offs.reshape(8, 16, -1).transpose(0, 2, 1).reshape(8, -1).astype(np.int64)


def pick8(x, idx, run):
    r = np.arange(len(x))
    return x[r[:, None], idx[r % (8 * run) // run]]


E2M1 = np.array([0.0, 0.5, 1.0, 1.5, 2.0, 3.0, 4.0, 6.0, -0.0, -0.5, -1.0, -1.5, -2.0, -3.0, -4.0, -6.0])


def pack_weight(w, fmt):
    k, n = w.shape
    w = f64(np.asarray(w, np.float32).astype(ml_dtypes.bfloat16)).reshape(k // 32, 32, n)
    amax = np.abs(w).max(1)
    if fmt == "e4m3":
        byte = np.frexp(amax)[1] - 1 + 127 - 7
    else:
        mant, ex = np.frexp(amax / 6.0)
        byte = np.where(mant > 0.5, ex, ex - 1) + 127
    byte = np.clip(np.where(amax > 0, byte, 1), 1, 254)
    scaled = (w * np.exp2(127.0 - byte)[:, None, :]).reshape(k, n).astype(np.float32)
    by_word = np.ascontiguousarray(scaled.reshape(k // 512, 128, 4, n).transpose(0, 1, 3, 2))
    if fmt == "e4m3":
        words = by_word.astype(ml_dtypes.float8_e4m3fn).view(np.uint8)
    else:
        c = by_word.astype(ml_dtypes.float4_e2m1fn).view(np.uint8) & 0xF
        words = (c[..., 0::2] | (c[..., 1::2] << 4)).reshape(k // 512, 128, 2 * n)
    return np.ascontiguousarray(words), np.ascontiguousarray(byte.astype(np.uint8).reshape(k // 512, 16, n))


def unpack_weight(words, scales, fmt):
    g, _, n = scales.shape
    words = np.ascontiguousarray(words).reshape(g, 128, n, -1)
    if fmt == "e4m3":
        vals = words.view(ml_dtypes.float8_e4m3fn).astype(np.float64)
    else:
        nib = np.empty((g, 128, n, 4), np.uint8)
        nib[..., 0::2] = words & 0xF
        nib[..., 1::2] = words >> 4
        vals = E2M1[nib]
    vals = vals * np.repeat(np.exp2(scales.astype(np.float64) - 127.0), 8, axis=1)[..., None]
    return vals.transpose(0, 1, 3, 2).reshape(g * 512, n)


D, K, T, I, Q = 512, 512, 1024, 512, 128


def setup_inputs():
    n = np.random.standard_normal
    idx = np.stack([np.random.permutation(T)[:I] for _ in range(8)])
    idx2 = np.stack([np.random.permutation(T)[:I] for _ in range(8)])
    idx3 = np.stack([np.random.permutation(T)[:I] for _ in range(8)])
    idx4 = np.stack([np.random.permutation(T)[:I] for _ in range(8)])
    fd = mx_kscale(D)
    fk = mx_kscale(K)
    wqp = pack_weight(n((D, K)) * 1.0 / np.sqrt(D) * fd[:, None] * fk, "e4m3")
    cachep = pack_weight(n((K, T)) * 1.0 / np.sqrt(K) / fk[:, None], "e2m1")
    tagsp = pack_weight(n((D, T)) * 0.5 / np.sqrt(D) * fd[:, None], "e4m3")
    return {
        "states": (n((D, Q)) * 0.95 / fd[:, None]).astype(np.float32),
        "wq_words": wqp[0],
        "wq_scales": wqp[1],
        "cache_words": cachep[0],
        "cache_scales": cachep[1],
        "tags_words": tagsp[0],
        "tags_scales": tagsp[1],
        "offs": striped8(idx),
        "offs2": striped8(idx2),
        "offs3": striped8(idx3),
        "offs4": striped8(idx4),
    }


def reference(states, wq_words, wq_scales, cache_words, cache_scales, tags_words, tags_scales, offs, offs2, offs3, offs4):
    idx = unstriped8(offs)
    idx2 = unstriped8(offs2)
    idx3 = unstriped8(offs3)
    idx4 = unstriped8(offs4)
    wqu = unpack_weight(wq_words, wq_scales, "e4m3")
    cacheu = unpack_weight(cache_words, cache_scales, "e2m1")
    tagsu = unpack_weight(tags_words, tags_scales, "e4m3")
    statesq = mxq(f64(states), 0, "e4m3")
    qv = wqu.T @ statesq
    qvq = mxq(qv, 0, "e4m3")
    a = qvq.T @ cacheu + statesq.T @ tagsu
    a1 = np.pad(a, ((0, 0), (512, 0)))[:, :T]
    f1 = np.zeros((Q, T))
    f1[np.arange(Q)[:, None], idx2[np.arange(Q) % 128 // 16]] = pick8(a1, idx, 16)
    c1 = np.maximum(a, f1)
    f2 = np.zeros((Q, T))
    f2[np.arange(Q)[:, None], idx4[np.arange(Q) % 128 // 16]] = pick8(c1, idx3, 16)
    c2 = c1 - f2
    y = pick8(c2, idx, 16)
    return y

@@ -1,0 +1,177 @@
+from contextlib import ExitStack
+
+import concourse.mybir as mybir
+
+D, K, T, I, Q = 512, 512, 1024, 512, 128
+FLOPS = 2 * D * K * Q + 2 * K * Q * T + 2 * D * Q * T
+
+F32 = mybir.dt.float32
+BF16 = mybir.dt.bfloat16
+I32 = mybir.dt.int32
+U32 = mybir.dt.uint32
+U16 = mybir.dt.uint16
+U8 = mybir.dt.uint8
+FP8X4 = mybir.dt.float8_e4m3fn_x4
+FP4X4 = mybir.dt.float4_e2m1fn_x4
+COPY = mybir.ActivationFunctionType.Copy
+MAX = mybir.AluOpType.max
+SUBTRACT = mybir.AluOpType.subtract
+
+P = 128
+PACK = 4
+HALF = T // 2
+QUARTER = T // 4
+PIECE = I // 2
+PIECE_COLS = PIECE // 16
+CAST_SPLIT = 96
+
+
+def load_scale_rows(nc, plane, scales):
+    rows = scales[0].bitcast(I32).rearrange("(g r) c -> r g c", r=4)
+    for r in range(4):
+        nc.sync.dma_start(plane[:].bitcast(I32)[r:P:32, :], rows[r])
+
+
+def tile_attend_halfaway_parts_kernel(tc, states, wq_words, wq_scales, cache_words, cache_scales, tags_words, tags_scales, offs, offs2, offs3, offs4, out):
+    nc = tc.nc
+    with ExitStack() as ctx:
+        sb = ctx.enter_context(tc.tile_pool(name="sb", bufs=1))
+        ps = ctx.enter_context(tc.psum_pool(name="ps", bufs=1))
+
+        wq_plane_in = sb.tile([P, K], U8, name="wq_plane_in", align_bytes=64)
+        tags_plane = sb.tile([P, T], U8, name="tags_plane", align_bytes=64)
+        cache_plane = sb.tile([P, T], U8, name="cache_plane", align_bytes=64)
+        for plane in (wq_plane_in, tags_plane, cache_plane):
+            nc.vector.memset(plane[:].bitcast(I32), 0)
+
+        states_raw = sb.tile([P, PACK, Q], F32, name="states_raw", align_bytes=64)
+        nc.sync.dma_start(states_raw[:], states.rearrange("(p j) q -> p j q", j=PACK))
+        load_scale_rows(nc, wq_plane_in, wq_scales)
+        wq_in = sb.tile([P, K], U32, name="wq_in", align_bytes=64)
+        nc.sync.dma_start(wq_in[:].bitcast(I32), wq_words[0].rearrange("p n t -> p (n t)").bitcast(I32))
+        tags_dram = tags_words[0].rearrange("p n t -> p (n t)").bitcast(I32)
+        cache_dram = cache_words[0].bitcast(I32)
+        tags = [sb.tile([P, HALF], U32, name="tags%d" % h, align_bytes=64) for h in range(2)]
+        cache = [sb.tile([P, 2 * HALF], U8, name="cache%d" % h, align_bytes=64) for h in range(2)]
+
+        def load_keys(h):
+            nc.sync.dma_start(tags[h][:].bitcast(I32), tags_dram[:, h * HALF : (h + 1) * HALF])
+            nc.sync.dma_start(cache[h][:].bitcast(I32), cache_dram[:, h * QUARTER : (h + 1) * QUARTER])
+
+        load_keys(0)
+        load_scale_rows(nc, tags_plane, tags_scales)
+        load_scale_rows(nc, cache_plane, cache_scales)
+        idx = sb.tile([P, I // 16], U16, name="idx")
+        idx2 = sb.tile([P, I // 16], U16, name="idx2")
+        idx3 = sb.tile([P, I // 16], U16, name="idx3")
+        idx4 = sb.tile([P, I // 16], U16, name="idx4")
+        nc.sync.dma_start(idx[:], offs)
+        nc.sync.dma_start(idx2[:], offs2)
+        load_keys(1)
+        nc.sync.dma_start(idx3[:], offs3)
+        nc.sync.dma_start(idx4[:], offs4)
+
+        a1 = sb.tile([P, T], F32, name="a1", tag="a1_then_f2", align_bytes=64)
+        f1 = sb.tile([P, T], F32, name="f1", align_bytes=64)
+        nc.vector.memset(a1[:, 0:HALF], 0.0)
+        nc.vector.memset(f1[:], 0.0)
+
+        states_bf = sb.tile([P, Q, PACK], BF16, name="states_bf", align_bytes=64)
+        states_qj = states_raw[:].rearrange("p j q -> p q j")
+        nc.vector.tensor_copy(states_bf[:, 0:CAST_SPLIT, :], states_qj[:, 0:CAST_SPLIT, :])
+        nc.scalar.activation(states_bf[:, CAST_SPLIT:Q, :], states_qj[:, CAST_SPLIT:Q, :], COPY)
+        wq_plane = sb.tile([P, K], U8, name="wq_plane", align_bytes=64)
+        nc.vector.tensor_copy(
+            wq_plane[:].rearrange("p (t m) -> p t m", t=PACK), wq_plane_in[:].rearrange("p (m t) -> p t m", t=PACK)
+        )
+        states_codes = sb.tile([P, Q], U32, name="states_codes", align_bytes=64)
+        states_plane = sb.tile([P, Q], U8, name="states_plane", align_bytes=64)
+        nc.vector.quantize_mx(states_codes[:].bitcast(FP8X4), states_plane[:], states_bf[:].rearrange("p q j -> p (q j)"))
+
+        wq = sb.tile([P, K], U32, name="wq", align_bytes=64)
+        nc.scalar.copy(wq[:].rearrange("p (t m) -> p m t", t=PACK), wq_in[:].rearrange("p (m t) -> p m t", t=PACK))
+
+        qv_bank = ps.tile([P, PACK, Q], F32, name="qv_bank")
+        for t in range(PACK):
+            cols = slice(t * P, (t + 1) * P)
+            nc.tensor.matmul_mx(
+                qv_bank[:, t, :],
+                lhsT=wq[:, cols].bitcast(FP8X4),
+                lhsT_scale=wq_plane[:, cols],
+                rhs=states_codes[:].bitcast(FP8X4),
+                rhs_scale=states_plane[:],
+                start=True,
+                stop=True,
+            )
+        qv_bf = sb.tile([P, Q, PACK], BF16, name="qv_bf", align_bytes=64)
+        nc.scalar.copy(qv_bf[:], qv_bank[:].rearrange("p t q -> p q t"))
+        qv_codes = sb.tile([P, Q], U32, name="qv_codes", align_bytes=64)
+        qv_plane = sb.tile([P, Q], U8, name="qv_plane", align_bytes=64)
+        nc.vector.quantize_mx(qv_codes[:].bitcast(FP8X4), qv_plane[:], qv_bf[:].rearrange("p q t -> p (q t)"))
+
+        spans = [(0, QUARTER), (QUARTER, HALF), (HALF, T)]
+        banks = [ps.tile([P, hi - lo], F32, name="a_bank%d" % lo) for lo, hi in spans]
+
+        def tags_pass(s):
+            lo, hi = spans[s]
+            h, first = divmod(lo, HALF)
+            nc.tensor.matmul_mx(
+                banks[s][:],
+                lhsT=states_codes[:].bitcast(FP8X4),
+                lhsT_scale=states_plane[:],
+                rhs=tags[h][:, first : first + hi - lo].bitcast(FP8X4),
+                rhs_scale=tags_plane[:, lo:hi],
+                start=True,
+                stop=False,
+            )
+
+        def cache_pass(s):
+            lo, hi = spans[s]
+            h, first = divmod(lo, HALF)
+            nc.tensor.matmul_mx(
+                banks[s][:],
+                lhsT=qv_codes[:].bitcast(FP8X4),
+                lhsT_scale=qv_plane[:],
+                rhs=cache[h][:, 2 * first : 2 * (first + hi - lo)].bitcast(FP4X4),
+                rhs_scale=cache_plane[:, lo:hi],
+                start=False,
+                stop=True,
+            )
+
+        tags_pass(0)
+        tags_pass(1)
+        cache_pass(0)
+        cache_pass(1)
+        tags_pass(2)
+        cache_pass(2)
+
+        nc.vector.tensor_copy(a1[:, HALF : HALF + QUARTER], banks[0][:])
+        nc.scalar.copy(a1[:, HALF + QUARTER : T], banks[1][:])
+
+        def gather(picked, window, offsets):
+            nc.vector.tensor_copy(picked[:, 0:PIECE], window[:].indirect(offsets[:, 0:PIECE_COLS]))
+            nc.scalar.activation(picked[:, PIECE:I], window[:].indirect(offsets[:, PIECE_COLS : 2 * PIECE_COLS]), COPY)
+
+        a1_picked = sb.tile([P, I], F32, name="a1_picked", align_bytes=64)
+        gather(a1_picked, a1, idx)
+        nc.scalar.activation(f1[:].indirect(idx2[:]), a1_picked[:], COPY)
+
+        f2 = sb.tile([P, T], F32, name="f2", tag="a1_then_f2", align_bytes=64)
+        nc.vector.memset(f2[:], 0.0)
+
+        c1 = sb.tile([P, T], F32, name="c1", align_bytes=64)
+        for s, (lo, hi) in enumerate(spans):
+            nc.vector.tensor_tensor(c1[:, lo:hi], f1[:, lo:hi], banks[s][:], MAX)
+
+        c1_picked = sb.tile([P, I], F32, name="c1_picked", align_bytes=64)
+        gather(c1_picked, c1, idx3)
+        nc.scalar.activation(f2[:].indirect(idx4[:]), c1_picked[:], COPY)
+
+        c2 = sb.tile([P, T], F32, name="c2", align_bytes=64)
+        nc.vector.tensor_tensor(c2[:], c1[:], f2[:], SUBTRACT)
+
+        c2_picked = sb.tile([P, I], F32, name="c2_picked", align_bytes=64)
+        gather(c2_picked, c2, idx)
+        for half in range(2):
+            cols = slice(half * PIECE, (half + 1) * PIECE)
+            nc.sync.dma_start(out[:, cols], c2_picked[:, cols])

@@ -39,8 +39,8 @@ def tile_attend_halfaway_parts_kernel(tc, states, wq_words, wq_scales, cache_wor
         ps = ctx.enter_context(tc.psum_pool(name="ps", bufs=1))
 
         wq_plane_in = sb.tile([P, K], U8, name="wq_plane_in", align_bytes=64)
-        tags_plane = sb.tile([P, T], U8, name="tags_plane", align_bytes=64)
         cache_plane = sb.tile([P, T], U8, name="cache_plane", align_bytes=64)
+        tags_plane = sb.tile([P, T], U8, name="tags_plane", align_bytes=64)
         for plane in (wq_plane_in, tags_plane, cache_plane):
             nc.vector.memset(plane[:].bitcast(I32), 0)
 
@@ -55,16 +55,16 @@ def tile_attend_halfaway_parts_kernel(tc, states, wq_words, wq_scales, cache_wor
         cache = [sb.tile([P, 2 * HALF], U8, name="cache%d" % h, align_bytes=64) for h in range(2)]
 
         def load_keys(h):
-            nc.sync.dma_start(tags[h][:].bitcast(I32), tags_dram[:, h * HALF : (h + 1) * HALF])
             nc.sync.dma_start(cache[h][:].bitcast(I32), cache_dram[:, h * QUARTER : (h + 1) * QUARTER])
+            nc.sync.dma_start(tags[h][:].bitcast(I32), tags_dram[:, h * HALF : (h + 1) * HALF])
 
-        load_keys(0)
-        load_scale_rows(nc, tags_plane, tags_scales)
-        load_scale_rows(nc, cache_plane, cache_scales)
         idx = sb.tile([P, I // 16], U16, name="idx")
         idx2 = sb.tile([P, I // 16], U16, name="idx2")
         idx3 = sb.tile([P, I // 16], U16, name="idx3")
         idx4 = sb.tile([P, I // 16], U16, name="idx4")
+        load_keys(0)
+        load_scale_rows(nc, tags_plane, tags_scales)
+        load_scale_rows(nc, cache_plane, cache_scales)
         nc.sync.dma_start(idx[:], offs)
         nc.sync.dma_start(idx2[:], offs2)
         load_keys(1)
@@ -80,24 +80,24 @@ def tile_attend_halfaway_parts_kernel(tc, states, wq_words, wq_scales, cache_wor
         states_qj = states_raw[:].rearrange("p j q -> p q j")
         nc.vector.tensor_copy(states_bf[:, 0:CAST_SPLIT, :], states_qj[:, 0:CAST_SPLIT, :])
         nc.scalar.activation(states_bf[:, CAST_SPLIT:Q, :], states_qj[:, CAST_SPLIT:Q, :], COPY)
-        wq_plane = sb.tile([P, K], U8, name="wq_plane", align_bytes=64)
-        nc.vector.tensor_copy(
-            wq_plane[:].rearrange("p (t m) -> p t m", t=PACK), wq_plane_in[:].rearrange("p (m t) -> p t m", t=PACK)
-        )
         states_codes = sb.tile([P, Q], U32, name="states_codes", align_bytes=64)
         states_plane = sb.tile([P, Q], U8, name="states_plane", align_bytes=64)
         nc.vector.quantize_mx(states_codes[:].bitcast(FP8X4), states_plane[:], states_bf[:].rearrange("p q j -> p (q j)"))
 
-        wq = sb.tile([P, K], U32, name="wq", align_bytes=64)
-        nc.scalar.copy(wq[:].rearrange("p (t m) -> p m t", t=PACK), wq_in[:].rearrange("p (m t) -> p m t", t=PACK))
+        wq = [sb.tile([P, 2, P], U32, name="wq%d" % u, align_bytes=64) for u in range(2)]
+        wq_plane = [sb.tile([P, 2, P], U8, name="wq_plane%d" % u, align_bytes=64) for u in range(2)]
+        for u in range(2):
+            places = slice(2 * u, 2 * u + 2)
+            nc.scalar.copy(wq[u][:].rearrange("p e m -> p m e"), wq_in[:].rearrange("p (m t) -> p m t", t=PACK)[:, :, places])
+            nc.vector.tensor_copy(wq_plane[u][:], wq_plane_in[:].rearrange("p (m t) -> p t m", t=PACK)[:, places, :])
 
         qv_bank = ps.tile([P, PACK, Q], F32, name="qv_bank")
         for t in range(PACK):
-            cols = slice(t * P, (t + 1) * P)
+            u, e = divmod(t, 2)
             nc.tensor.matmul_mx(
                 qv_bank[:, t, :],
-                lhsT=wq[:, cols].bitcast(FP8X4),
-                lhsT_scale=wq_plane[:, cols],
+                lhsT=wq[u][:, e, :].bitcast(FP8X4),
+                lhsT_scale=wq_plane[u][:, e, :],
                 rhs=states_codes[:].bitcast(FP8X4),
                 rhs_scale=states_plane[:],
                 start=True,
@@ -109,10 +109,10 @@ def tile_attend_halfaway_parts_kernel(tc, states, wq_words, wq_scales, cache_wor
         qv_plane = sb.tile([P, Q], U8, name="qv_plane", align_bytes=64)
         nc.vector.quantize_mx(qv_codes[:].bitcast(FP8X4), qv_plane[:], qv_bf[:].rearrange("p q t -> p (q t)"))
 
-        spans = [(0, QUARTER), (QUARTER, HALF), (HALF, T)]
+        spans = [(0, QUARTER), (QUARTER, QUARTER + P), (QUARTER + P, HALF), (HALF, T)]
         banks = [ps.tile([P, hi - lo], F32, name="a_bank%d" % lo) for lo, hi in spans]
 
-        def tags_pass(s):
+        def tags_pass(s, first_pass):
             lo, hi = spans[s]
             h, first = divmod(lo, HALF)
             nc.tensor.matmul_mx(
@@ -121,11 +121,11 @@ def tile_attend_halfaway_parts_kernel(tc, states, wq_words, wq_scales, cache_wor
                 lhsT_scale=states_plane[:],
                 rhs=tags[h][:, first : first + hi - lo].bitcast(FP8X4),
                 rhs_scale=tags_plane[:, lo:hi],
-                start=True,
-                stop=False,
+                start=first_pass,
+                stop=not first_pass,
             )
 
-        def cache_pass(s):
+        def cache_pass(s, first_pass):
             lo, hi = spans[s]
             h, first = divmod(lo, HALF)
             nc.tensor.matmul_mx(
@@ -134,19 +134,20 @@ def tile_attend_halfaway_parts_kernel(tc, states, wq_words, wq_scales, cache_wor
                 lhsT_scale=qv_plane[:],
                 rhs=cache[h][:, 2 * first : 2 * (first + hi - lo)].bitcast(FP4X4),
                 rhs_scale=cache_plane[:, lo:hi],
-                start=False,
-                stop=True,
+                start=first_pass,
+                stop=not first_pass,
             )
 
-        tags_pass(0)
-        tags_pass(1)
-        cache_pass(0)
-        cache_pass(1)
-        tags_pass(2)
-        cache_pass(2)
+        for s in range(3):
+            tags_pass(s, True)
+        for s in range(3):
+            cache_pass(s, False)
+        cache_pass(3, True)
+        tags_pass(3, False)
 
-        nc.vector.tensor_copy(a1[:, HALF : HALF + QUARTER], banks[0][:])
-        nc.scalar.copy(a1[:, HALF + QUARTER : T], banks[1][:])
+        for s, copy in enumerate((nc.vector.tensor_copy, nc.scalar.copy, nc.vector.tensor_copy)):
+            lo, hi = spans[s]
+            copy(a1[:, HALF + lo : HALF + hi], banks[s][:])
 
         def gather(picked, window, offsets):
             nc.vector.tensor_copy(picked[:, 0:PIECE], window[:].indirect(offsets[:, 0:PIECE_COLS]))

from contextlib import ExitStack

import concourse.mybir as mybir

D, K, T, I, Q = 512, 512, 1024, 512, 128
FLOPS = 2 * D * K * Q + 2 * K * Q * T + 2 * D * Q * T

F32 = mybir.dt.float32
BF16 = mybir.dt.bfloat16
I32 = mybir.dt.int32
U32 = mybir.dt.uint32
U16 = mybir.dt.uint16
U8 = mybir.dt.uint8
FP8X4 = mybir.dt.float8_e4m3fn_x4
FP4X4 = mybir.dt.float4_e2m1fn_x4
COPY = mybir.ActivationFunctionType.Copy
MAX = mybir.AluOpType.max
SUBTRACT = mybir.AluOpType.subtract

P = 128
PACK = 4
HALF = T // 2
QUARTER = T // 4
PIECE = I // 2
PIECE_COLS = PIECE // 16
CAST_SPLIT = 96


def load_scale_rows(nc, plane, scales):
    rows = scales[0].bitcast(I32).rearrange("(g r) c -> r g c", r=4)
    for r in range(4):
        nc.sync.dma_start(plane[:].bitcast(I32)[r:P:32, :], rows[r])


def tile_attend_halfaway_parts_kernel(tc, states, wq_words, wq_scales, cache_words, cache_scales, tags_words, tags_scales, offs, offs2, offs3, offs4, out):
    nc = tc.nc
    with ExitStack() as ctx:
        sb = ctx.enter_context(tc.tile_pool(name="sb", bufs=1))
        ps = ctx.enter_context(tc.psum_pool(name="ps", bufs=1))

        wq_plane_in = sb.tile([P, K], U8, name="wq_plane_in", align_bytes=64)
        cache_plane = sb.tile([P, T], U8, name="cache_plane", align_bytes=64)
        tags_plane = sb.tile([P, T], U8, name="tags_plane", align_bytes=64)
        for plane in (wq_plane_in, tags_plane, cache_plane):
            nc.vector.memset(plane[:].bitcast(I32), 0)

        states_raw = sb.tile([P, PACK, Q], F32, name="states_raw", align_bytes=64)
        nc.sync.dma_start(states_raw[:], states.rearrange("(p j) q -> p j q", j=PACK))
        load_scale_rows(nc, wq_plane_in, wq_scales)
        wq_in = sb.tile([P, K], U32, name="wq_in", align_bytes=64)
        nc.sync.dma_start(wq_in[:].bitcast(I32), wq_words[0].rearrange("p n t -> p (n t)").bitcast(I32))
        tags_dram = tags_words[0].rearrange("p n t -> p (n t)").bitcast(I32)
        cache_dram = cache_words[0].bitcast(I32)
        tags = [sb.tile([P, HALF], U32, name="tags%d" % h, align_bytes=64) for h in range(2)]
        cache = [sb.tile([P, 2 * HALF], U8, name="cache%d" % h, align_bytes=64) for h in range(2)]

        def load_keys(h):
            nc.sync.dma_start(cache[h][:].bitcast(I32), cache_dram[:, h * QUARTER : (h + 1) * QUARTER])
            nc.sync.dma_start(tags[h][:].bitcast(I32), tags_dram[:, h * HALF : (h + 1) * HALF])

        idx = sb.tile([P, I // 16], U16, name="idx")
        idx2 = sb.tile([P, I // 16], U16, name="idx2")
        idx3 = sb.tile([P, I // 16], U16, name="idx3")
        idx4 = sb.tile([P, I // 16], U16, name="idx4")
        load_keys(0)
        load_scale_rows(nc, tags_plane, tags_scales)
        load_scale_rows(nc, cache_plane, cache_scales)
        nc.sync.dma_start(idx[:], offs)
        nc.sync.dma_start(idx2[:], offs2)
        load_keys(1)
        nc.sync.dma_start(idx3[:], offs3)
        nc.sync.dma_start(idx4[:], offs4)

        a1 = sb.tile([P, T], F32, name="a1", tag="a1_then_f2", align_bytes=64)
        f1 = sb.tile([P, T], F32, name="f1", align_bytes=64)
        nc.vector.memset(a1[:, 0:HALF], 0.0)
        nc.vector.memset(f1[:], 0.0)

        states_bf = sb.tile([P, Q, PACK], BF16, name="states_bf", align_bytes=64)
        states_qj = states_raw[:].rearrange("p j q -> p q j")
        nc.vector.tensor_copy(states_bf[:, 0:CAST_SPLIT, :], states_qj[:, 0:CAST_SPLIT, :])
        nc.scalar.activation(states_bf[:, CAST_SPLIT:Q, :], states_qj[:, CAST_SPLIT:Q, :], COPY)
        states_codes = sb.tile([P, Q], U32, name="states_codes", align_bytes=64)
        states_plane = sb.tile([P, Q], U8, name="states_plane", align_bytes=64)
        nc.vector.quantize_mx(states_codes[:].bitcast(FP8X4), states_plane[:], states_bf[:].rearrange("p q j -> p (q j)"))

        wq = [sb.tile([P, 2, P], U32, name="wq%d" % u, align_bytes=64) for u in range(2)]
        wq_plane = [sb.tile([P, 2, P], U8, name="wq_plane%d" % u, align_bytes=64) for u in range(2)]
        for u in range(2):
            places = slice(2 * u, 2 * u + 2)
            nc.scalar.copy(wq[u][:].rearrange("p e m -> p m e"), wq_in[:].rearrange("p (m t) -> p m t", t=PACK)[:, :, places])
            nc.vector.tensor_copy(wq_plane[u][:], wq_plane_in[:].rearrange("p (m t) -> p t m", t=PACK)[:, places, :])

        qv_bank = ps.tile([P, PACK, Q], F32, name="qv_bank")
        for t in range(PACK):
            u, e = divmod(t, 2)
            nc.tensor.matmul_mx(
                qv_bank[:, t, :],
                lhsT=wq[u][:, e, :].bitcast(FP8X4),
                lhsT_scale=wq_plane[u][:, e, :],
                rhs=states_codes[:].bitcast(FP8X4),
                rhs_scale=states_plane[:],
                start=True,
                stop=True,
            )
        qv_bf = sb.tile([P, Q, PACK], BF16, name="qv_bf", align_bytes=64)
        nc.scalar.copy(qv_bf[:], qv_bank[:].rearrange("p t q -> p q t"))
        qv_codes = sb.tile([P, Q], U32, name="qv_codes", align_bytes=64)
        qv_plane = sb.tile([P, Q], U8, name="qv_plane", align_bytes=64)
        nc.vector.quantize_mx(qv_codes[:].bitcast(FP8X4), qv_plane[:], qv_bf[:].rearrange("p q t -> p (q t)"))

        spans = [(0, QUARTER), (QUARTER, QUARTER + P), (QUARTER + P, HALF), (HALF, T)]
        banks = [ps.tile([P, hi - lo], F32, name="a_bank%d" % lo) for lo, hi in spans]

        def tags_pass(s, first_pass):
            lo, hi = spans[s]
            h, first = divmod(lo, HALF)
            nc.tensor.matmul_mx(
                banks[s][:],
                lhsT=states_codes[:].bitcast(FP8X4),
                lhsT_scale=states_plane[:],
                rhs=tags[h][:, first : first + hi - lo].bitcast(FP8X4),
                rhs_scale=tags_plane[:, lo:hi],
                start=first_pass,
                stop=not first_pass,
            )

        def cache_pass(s, first_pass):
            lo, hi = spans[s]
            h, first = divmod(lo, HALF)
            nc.tensor.matmul_mx(
                banks[s][:],
                lhsT=qv_codes[:].bitcast(FP8X4),
                lhsT_scale=qv_plane[:],
                rhs=cache[h][:, 2 * first : 2 * (first + hi - lo)].bitcast(FP4X4),
                rhs_scale=cache_plane[:, lo:hi],
                start=first_pass,
                stop=not first_pass,
            )

        for s in range(3):
            tags_pass(s, True)
        for s in range(3):
            cache_pass(s, False)
        cache_pass(3, True)
        tags_pass(3, False)

        for s, copy in enumerate((nc.vector.tensor_copy, nc.scalar.copy, nc.vector.tensor_copy)):
            lo, hi = spans[s]
            copy(a1[:, HALF + lo : HALF + hi], banks[s][:])

        def gather(picked, window, offsets):
            nc.vector.tensor_copy(picked[:, 0:PIECE], window[:].indirect(offsets[:, 0:PIECE_COLS]))
            nc.scalar.activation(picked[:, PIECE:I], window[:].indirect(offsets[:, PIECE_COLS : 2 * PIECE_COLS]), COPY)

        a1_picked = sb.tile([P, I], F32, name="a1_picked", align_bytes=64)
        gather(a1_picked, a1, idx)
        nc.scalar.activation(f1[:].indirect(idx2[:]), a1_picked[:], COPY)

        f2 = sb.tile([P, T], F32, name="f2", tag="a1_then_f2", align_bytes=64)
        nc.vector.memset(f2[:], 0.0)

        c1 = sb.tile([P, T], F32, name="c1", align_bytes=64)
        for s, (lo, hi) in enumerate(spans):
            nc.vector.tensor_tensor(c1[:, lo:hi], f1[:, lo:hi], banks[s][:], MAX)

        c1_picked = sb.tile([P, I], F32, name="c1_picked", align_bytes=64)
        gather(c1_picked, c1, idx3)
        nc.scalar.activation(f2[:].indirect(idx4[:]), c1_picked[:], COPY)

        c2 = sb.tile([P, T], F32, name="c2", align_bytes=64)
        nc.vector.tensor_tensor(c2[:], c1[:], f2[:], SUBTRACT)

        c2_picked = sb.tile([P, I], F32, name="c2_picked", align_bytes=64)
        gather(c2_picked, c2, idx)
        for half in range(2):
            cols = slice(half * PIECE, (half + 1) * PIECE)
            nc.sync.dma_start(out[:, cols], c2_picked[:, cols])
